import numpy as np
import ml_dtypes


def mxq(x, axis, fmt="e4m3"):
    dtype, down = {"e4m3": (ml_dtypes.float8_e4m3fn, 7), "e5m2": (ml_dtypes.float8_e5m2, 14)}[fmt]
    v = np.moveaxis(np.asarray(x, np.float32).astype(ml_dtypes.bfloat16).astype(np.float64), axis, -1)
    blocks = v.reshape(v.shape[:-1] + (-1, 32))
    amax = np.abs(blocks).max(-1, keepdims=True)
    byte = np.maximum(np.where(amax > 0, np.frexp(amax)[1] - 1 + 127, 0) - down, 1)
    scale = np.exp2(byte - 127.0)
    codes = (blocks / scale).astype(np.float32).astype(dtype).astype(np.float64)
    return np.moveaxis((codes * scale).reshape(v.shape), -1, axis)


WIDE = False


def mx_kscale(k):
    if not WIDE:
        return np.ones(k)
    levels = np.array([10, -10, 5, -5, 0])
    if k % 512:
        return np.exp2(np.random.permutation(np.resize(levels, k // 32))).repeat(32)
    a = np.empty((k // 512, 16))
    for p in range(k // 512):
        a[p, :8] = np.random.permutation(np.resize(levels, 8))
        for g in range(8):
            far = levels[np.abs(levels - a[p, g]) >= 10]
            a[p, g + 8] = far[np.random.randint(len(far))]
    return np.exp2(a.ravel()).repeat(32)


def f64(x):
    return np.asarray(x).astype(np.float64)


def striped(idx):
    return np.tile(idx.reshape(-1, 16).T, (8, 1)).astype(np.uint16)


def unstriped(offs):
    return offs[:16].T.reshape(-1).astype(np.int64)


def pack_weight(w):
    k, n = w.shape
    w = f64(np.asarray(w, np.float32).astype(ml_dtypes.bfloat16)).reshape(k // 32, 32, n)
    amax = np.abs(w).max(1)
    byte = np.clip(np.where(amax > 0, np.frexp(amax)[1] - 1 + 127 - 7, 1), 1, 254)
    scaled = (w * np.exp2(127.0 - byte)[:, None, :]).reshape(k, n).astype(np.float32)
    words = np.ascontiguousarray(scaled.reshape(k // 512, 128, 4, n).transpose(0, 1, 3, 2)).astype(ml_dtypes.float8_e4m3fn).view(np.uint8)
    return words, np.ascontiguousarray(byte.astype(np.uint8).reshape(k // 512, 16, n))


def unpack_weight(words, scales):
    g, p, n, _ = words.shape
    vals = np.ascontiguousarray(words).view(ml_dtypes.float8_e4m3fn).astype(np.float64) * np.repeat(np.exp2(scales.astype(np.float64) - 127.0), 8, axis=1)[..., None]
    return vals.transpose(0, 1, 3, 2).reshape(g * 512, n)


K, T, D, S, V, N = 1024, 512, 3, 768, 256, 512
P = 2 ** 7


def setup_inputs():
    n = np.random.standard_normal
    s = mx_kscale(K)[:, None]
    words, scales = pack_weight(n((K, N)) / np.sqrt(K) / s)
    return {
        "xT": (n((K, T)) * s / np.sqrt(D)).astype(ml_dtypes.bfloat16).astype(np.float32),
        "w_words": words,
        "w_scales": scales,
        "b": (0.3 * n((N, 1))).astype(np.float32),
        "gate": np.tile(np.random.uniform(0.5, 1.5, (D, 1, V)), (1, P, 1)).astype(ml_dtypes.bfloat16).astype(np.float32),
        "offs": striped(np.concatenate([np.random.permutation(T)[:V] for _ in range(D)])),
    }


def reference(xT, w_words, w_scales, b, gate, offs):
    w = unpack_weight(w_words, w_scales)
    idx = unstriped(offs)
    x = sum(f64(gate)[d, :1] * f64(xT)[:, idx[d * V:(d + 1) * V]] for d in range(D))
    return (w.T @ mxq(x, 0, "e4m3")) + f64(b)

@@ -1,0 +1,177 @@
+from contextlib import ExitStack
+
+import concourse.mybir as mybir
+from concourse.masks import make_identity
+
+K, T, D, V, N = 1024, 512, 3, 256, 512
+FLOPS = 2 * K * N * V
+
+F32 = mybir.dt.float32
+BF16 = mybir.dt.bfloat16
+I32 = mybir.dt.int32
+U32 = mybir.dt.uint32
+U16 = mybir.dt.uint16
+U8 = mybir.dt.uint8
+FP8X4 = mybir.dt.float8_e4m3fn_x4
+COPY = mybir.ActivationFunctionType.Copy
+IDENT = mybir.ActivationFunctionType.Identity
+MULT = mybir.AluOpType.mult
+ADD = mybir.AluOpType.add
+
+P = 128
+PASSES = 2
+PAIRS = 4
+PIECE = 384
+BIAS_ROW = 8
+CAST = ["v","s","s","s"]
+SCALE = ["ssssss","ssssss","svsvsv","svsvsv"]
+
+
+def tile_picked_bag_lin_bias_sub_l_kernel(tc, xT, w_words, w_scales, b, gate, offs, out):
+    nc = tc.nc
+    with ExitStack() as ctx:
+        keep = ctx.enter_context(tc.tile_pool(name="keep", bufs=1))
+        turn = ctx.enter_context(tc.psum_pool(name="turn", bufs=4))
+        back = ctx.enter_context(tc.psum_pool(name="back", bufs=4))
+
+        offsets = keep.tile([P, D * V // 16], U16, name="offsets")
+        raw = [keep.tile([P, 2, T], F32, name=f"raw{q}") for q in range(PAIRS)]
+        x_rows = xT.rearrange("(a p u e) t -> a u p e t", a=PASSES, p=P, u=2, e=2)
+        nc.sync.dma_start(raw[0][:], x_rows[0, 0])
+        nc.sync.dma_start(offsets[:], offs)
+        for q in range(1, PAIRS):
+            nc.sync.dma_start(raw[q][:], x_rows[q // 2, q % 2])
+
+        rows = keep.tile([P, P], F32, name="rows")
+        nc.vector.memset(rows[:], 0.0)
+        nc.scalar.dma_start(rows[0 : 2 * D, :], gate[:, 0, :].rearrange("d (h v) -> d h v", h=2))
+        nc.scalar.dma_start(rows[BIAS_ROW : BIAS_ROW + 4, :], b.rearrange("(t p) o -> t (p o)", p=P))
+        ident = keep.tile([P, P], F32, name="ident")
+        make_identity(nc, ident[:])
+        w_plane = keep.tile([P, N], U8, name="w_plane", align_bytes=64)
+        nc.gpsimd.memset(w_plane[:].bitcast(U32), 0)
+
+        warm = keep.tile([P, 8], F32, name="warm")
+        nc.vector.memset(warm[:, 0:4], 0.0)
+        nc.scalar.activation(warm[:, 4:8], warm[:, 0:4], IDENT)
+
+        w_codes = keep.tile([P, PASSES, N], U32, name="w_codes", align_bytes=64)
+        nc.sync.dma_start(w_codes[:].bitcast(I32), w_words.rearrange("a p n t -> p a (n t)").bitcast(I32))
+        for quad in range(4):
+            nc.sync.dma_start(
+                w_plane[32 * quad : 32 * quad + 8, :].bitcast(I32),
+                w_scales[:, 4 * quad : 4 * quad + 4, :].bitcast(I32),
+            )
+
+        rows_turned = turn.tile([P, 4, P], F32, name="turned")
+        nc.tensor.transpose(rows_turned[:, 0, :], rows[:], ident[:])
+        cols = keep.tile([P, 16], F32, name="cols")
+        nc.scalar.copy(cols[:], rows_turned[:, 0, 0:16])
+
+        pairs = [keep.tile([P, T, 2], BF16, name=f"pairs{q}") for q in range(PAIRS)]
+        picked = [[keep.tile([P, PIECE], U32, name=f"picked{q}_{s}") for s in range(2)] for q in range(PAIRS)]
+        scaled = [[keep.tile([P, 2, P], F32, name=f"scaled{q}_{c}") for c in range(2 * D)] for q in range(PAIRS)]
+        sums = [[None, None] for a in range(PASSES)]
+        x_bf = [keep.tile([P, V, 4], BF16, name=f"x_bf{a}", align_bytes=64) for a in range(PASSES)]
+        x_codes = [keep.tile([P, V], U32, name=f"x_codes{a}", align_bytes=64) for a in range(PASSES)]
+        x_plane = [keep.tile([P, V], U8, name=f"x_plane{a}", align_bytes=64) for a in range(PASSES)]
+
+        def cast(q):
+            src = raw[q][:].rearrange("p e t -> p t e")
+            if CAST[q] == "v":
+                nc.vector.tensor_copy(pairs[q][:], src)
+            elif CAST[q] == "s":
+                nc.scalar.copy(pairs[q][:], src)
+            else:
+                nc.gpsimd.tensor_scalar(pairs[q][:], src, 1.0, 0.0, MULT, ADD)
+
+        def gather(q):
+            window = pairs[q][:].rearrange("p t e -> p (t e)").bitcast(U32)
+            for s in range(2):
+                nc.vector.tensor_copy(picked[q][s][:], window.indirect(offsets[:, 24 * s : 24 * s + 24]))
+
+        def weigh(q):
+            for s in range(2):
+                turned = turn.tile([P, 4, P], F32, name="turned")
+                for i in range(3):
+                    nc.tensor.transpose(turned[:, i, :], picked[q][s][:, P * i : P * (i + 1)].bitcast(F32), ident[:])
+                for i in range(3):
+                    c = 3 * s + i
+                    src = turned[:, i, :].bitcast(BF16).rearrange("v (p e) -> v e p", e=2)
+                    if SCALE[q][c] == "s":
+                        nc.scalar.activation(scaled[q][c][:], src, COPY, scale=cols[:, c : c + 1])
+                    else:
+                        nc.vector.tensor_scalar(scaled[q][c][:], src, cols[:, c : c + 1], None, MULT)
+
+        def add_up(q):
+            a, u = divmod(q, 2)
+            for h in range(2):
+                if u == 0:
+                    sums[a][h] = back.tile([P, 4, P], F32, name="sums")
+                for e in range(2):
+                    for d in range(D):
+                        nc.tensor.matmul(
+                            sums[a][h][:, 2 * u + e, :], scaled[q][2 * d + h][:, e, :], ident[:],
+                            start=(d == 0), stop=(d == D - 1), is_transpose=True,
+                        )
+
+        def round_sums(a):
+            nc.scalar.copy(x_bf[a][:, 0:P, :], sums[a][0][:].rearrange("p j v -> p v j"))
+            src = sums[a][1][:].rearrange("p j v -> p v j")
+            if a == 0:
+                nc.scalar.copy(x_bf[a][:, P:V, :], src)
+            else:
+                nc.vector.tensor_copy(x_bf[a][:, P:V, :], src)
+
+        def quantise(a):
+            nc.vector.quantize_mx(
+                out=x_codes[a][:].bitcast(FP8X4), scales=x_plane[a][:], in_=x_bf[a][:].rearrange("p v j -> p (v j)")
+            )
+
+        acc = [None] * 4
+
+        def multiply(a):
+            for t in range(4):
+                if a == 0:
+                    acc[t] = turn.tile([P, 4, P], F32, name="turned")
+                nc.tensor.matmul_mx(
+                    out=acc[t][:, 0:2, :].rearrange("p h v -> p (h v)"),
+                    lhsT=w_codes[:, a, P * t : P * (t + 1)].bitcast(FP8X4),
+                    lhsT_scale=w_plane[4 * a :, P * t : P * (t + 1)],
+                    rhs=x_codes[a][:].bitcast(FP8X4),
+                    rhs_scale=x_plane[a][:],
+                    start=(a == 0),
+                    stop=(a == PASSES - 1),
+                )
+
+        cast(0)
+        gather(0)
+        cast(1)
+        gather(1)
+        cast(2)
+        weigh(0)
+        gather(2)
+        cast(3)
+        add_up(0)
+        weigh(1)
+        gather(3)
+        add_up(1)
+        weigh(2)
+        round_sums(0)
+        add_up(2)
+        weigh(3)
+        quantise(0)
+        add_up(3)
+        multiply(0)
+        round_sums(1)
+        quantise(1)
+        multiply(1)
+        for t in range(4):
+            result = keep.tile([P, V], F32, name=f"result{t}")
+            src = acc[t][:, 0:2, :].rearrange("p h v -> p (h v)")
+            bias = cols[:, BIAS_ROW + t : BIAS_ROW + t + 1]
+            if t % 2 == 0:
+                nc.scalar.activation(result[:], src, IDENT, bias=bias)
+            else:
+                nc.vector.tensor_scalar(result[:], src, bias, None, ADD)
+            nc.sync.dma_start(out[P * t : P * (t + 1), :], result[:])

@@ -23,8 +23,8 @@ PASSES = 2
 PAIRS = 4
 PIECE = 384
 BIAS_ROW = 8
-CAST = ["v","s","s","s"]
-SCALE = ["ssssss","ssssss","svsvsv","svsvsv"]
+CAST = ["v","g","g","g"]
+SCALE = ["ssssss","ssssss","ssssss","ssmmms"]
 
 
 def tile_picked_bag_lin_bias_sub_l_kernel(tc, xT, w_words, w_scales, b, gate, offs, out):
@@ -39,13 +39,13 @@ def tile_picked_bag_lin_bias_sub_l_kernel(tc, xT, w_words, w_scales, b, gate, of
         x_rows = xT.rearrange("(a p u e) t -> a u p e t", a=PASSES, p=P, u=2, e=2)
         nc.sync.dma_start(raw[0][:], x_rows[0, 0])
         nc.sync.dma_start(offsets[:], offs)
+        rows = keep.tile([P, P], F32, name="rows")
+        nc.vector.memset(rows[:], 0.0)
+        nc.sync.dma_start(rows[0 : 2 * D, :], gate[:, 0, :].rearrange("d (h v) -> d h v", h=2))
+        nc.sync.dma_start(rows[BIAS_ROW : BIAS_ROW + 4, :], b.rearrange("(t p) o -> t (p o)", p=P))
         for q in range(1, PAIRS):
             nc.sync.dma_start(raw[q][:], x_rows[q // 2, q % 2])
 
-        rows = keep.tile([P, P], F32, name="rows")
-        nc.vector.memset(rows[:], 0.0)
-        nc.scalar.dma_start(rows[0 : 2 * D, :], gate[:, 0, :].rearrange("d (h v) -> d h v", h=2))
-        nc.scalar.dma_start(rows[BIAS_ROW : BIAS_ROW + 4, :], b.rearrange("(t p) o -> t (p o)", p=P))
         ident = keep.tile([P, P], F32, name="ident")
         make_identity(nc, ident[:])
         w_plane = keep.tile([P, N], U8, name="w_plane", align_bytes=64)
@@ -100,28 +100,30 @@ def tile_picked_bag_lin_bias_sub_l_kernel(tc, xT, w_words, w_scales, b, gate, of
                     src = turned[:, i, :].bitcast(BF16).rearrange("v (p e) -> v e p", e=2)
                     if SCALE[q][c] == "s":
                         nc.scalar.activation(scaled[q][c][:], src, COPY, scale=cols[:, c : c + 1])
-                    else:
+                    elif SCALE[q][c] == "v":
                         nc.vector.tensor_scalar(scaled[q][c][:], src, cols[:, c : c + 1], None, MULT)
+                    else:
+                        nc.vector.scalar_tensor_tensor(
+                            scaled[q][c][:], src, cols[:, c : c + 1], scaled[q][c - 2][:], MULT, ADD
+                        )
 
         def add_up(q):
             a, u = divmod(q, 2)
             for h in range(2):
                 if u == 0:
                     sums[a][h] = back.tile([P, 4, P], F32, name="sums")
+                terms = [d for d in range(D) if d == D - 1 or SCALE[q][2 * d + 2 + h] != "m"]
                 for e in range(2):
-                    for d in range(D):
+                    for d in terms:
                         nc.tensor.matmul(
                             sums[a][h][:, 2 * u + e, :], scaled[q][2 * d + h][:, e, :], ident[:],
-                            start=(d == 0), stop=(d == D - 1), is_transpose=True,
+                            start=(d == terms[0]), stop=(d == terms[-1]), is_transpose=True,
                         )
 
         def round_sums(a):
             nc.scalar.copy(x_bf[a][:, 0:P, :], sums[a][0][:].rearrange("p j v -> p v j"))
             src = sums[a][1][:].rearrange("p j v -> p v j")
-            if a == 0:
-                nc.scalar.copy(x_bf[a][:, P:V, :], src)
-            else:
-                nc.vector.tensor_copy(x_bf[a][:, P:V, :], src)
+            nc.vector.tensor_copy(x_bf[a][:, P:V, :], src)
 
         def quantise(a):
             nc.vector.quantize_mx(
@@ -149,19 +151,19 @@ def tile_picked_bag_lin_bias_sub_l_kernel(tc, xT, w_words, w_scales, b, gate, of
         cast(1)
         gather(1)
         cast(2)
-        weigh(0)
         gather(2)
         cast(3)
-        add_up(0)
-        weigh(1)
         gather(3)
-        add_up(1)
+        weigh(0)
+        weigh(1)
         weigh(2)
-        round_sums(0)
-        add_up(2)
         weigh(3)
-        quantise(0)
+        add_up(0)
+        add_up(1)
+        add_up(2)
+        round_sums(0)
         add_up(3)
+        quantise(0)
         multiply(0)
         round_sums(1)
         quantise(1)

@@ -23,27 +23,43 @@ PASSES = 2
 PAIRS = 4
 PIECE = 384
 BIAS_ROW = 8
-CAST = ["v","g","g","g"]
-SCALE = ["ssssss","ssssss","ssssss","ssmmms"]
+CAST = "vsss"
+SCALE = ["sssmsm","sssmsm","sssmsm","sssmmm"]
+WORDS = [[0,1],[0,1]]
+ROUND = ["sv","ss"]
+TURN_BANK = [[0,1],[2,4],[5,6],[7,0]]
+SUM_BANK = [[3,5],[2,4]]
+ACC_BANK = [[7,1,3,6],[0,5,2,4]]
+WARM_BANK = 7
+WARM_UP = 20
+FILL = [[2,2],[2,0],[0,0],[0,0]]
+N_MULTIPLY = 4
 
 
 def tile_picked_bag_lin_bias_sub_l_kernel(tc, xT, w_words, w_scales, b, gate, offs, out):
     nc = tc.nc
     with ExitStack() as ctx:
         keep = ctx.enter_context(tc.tile_pool(name="keep", bufs=1))
-        turn = ctx.enter_context(tc.psum_pool(name="turn", bufs=4))
-        back = ctx.enter_context(tc.psum_pool(name="back", bufs=4))
+        psum = ctx.enter_context(tc.psum_pool(name="psum", bufs=1))
+
+        def bank(i):
+            return psum.tile([P, 4, P], F32, name=f"bank{i}")
 
         offsets = keep.tile([P, D * V // 16], U16, name="offsets")
-        raw = [keep.tile([P, 2, T], F32, name=f"raw{q}") for q in range(PAIRS)]
         x_rows = xT.rearrange("(a p u e) t -> a u p e t", a=PASSES, p=P, u=2, e=2)
-        nc.sync.dma_start(raw[0][:], x_rows[0, 0])
+        first = [keep.tile([P, 2, T // 2], F32, name=f"first{i}") for i in range(2)]
+        for i in range(2):
+            nc.sync.dma_start(first[i][:], x_rows[0, 0][:, :, i * T // 2 : (i + 1) * T // 2])
         nc.sync.dma_start(offsets[:], offs)
         rows = keep.tile([P, P], F32, name="rows")
         nc.vector.memset(rows[:], 0.0)
-        nc.sync.dma_start(rows[0 : 2 * D, :], gate[:, 0, :].rearrange("d (h v) -> d h v", h=2))
+        gate_rows = gate[:, 0, :].rearrange("d (h v) -> d h v", h=2)
+        raw = [None] + [keep.tile([P, 2, T], F32, name=f"raw{q}") for q in range(1, PAIRS)]
+        nc.sync.dma_start(raw[1][:], x_rows[0, 1])
+        nc.sync.dma_start(rows[0:4, :], gate_rows[0:2])
+        nc.sync.dma_start(rows[4:6, :], gate_rows[2])
         nc.sync.dma_start(rows[BIAS_ROW : BIAS_ROW + 4, :], b.rearrange("(t p) o -> t (p o)", p=P))
-        for q in range(1, PAIRS):
+        for q in range(2, PAIRS):
             nc.sync.dma_start(raw[q][:], x_rows[q // 2, q % 2])
 
         ident = keep.tile([P, P], F32, name="ident")
@@ -63,20 +79,35 @@ def tile_picked_bag_lin_bias_sub_l_kernel(tc, xT, w_words, w_scales, b, gate, of
                 w_scales[:, 4 * quad : 4 * quad + 4, :].bitcast(I32),
             )
 
-        rows_turned = turn.tile([P, 4, P], F32, name="turned")
+        rows_turned = bank(WARM_BANK)
+        for i in range(WARM_UP):
+            nc.tensor.transpose(rows_turned[:, 1 + i % 3, :], ident[:], ident[:])
         nc.tensor.transpose(rows_turned[:, 0, :], rows[:], ident[:])
         cols = keep.tile([P, 16], F32, name="cols")
         nc.scalar.copy(cols[:], rows_turned[:, 0, 0:16])
 
         pairs = [keep.tile([P, T, 2], BF16, name=f"pairs{q}") for q in range(PAIRS)]
         picked = [[keep.tile([P, PIECE], U32, name=f"picked{q}_{s}") for s in range(2)] for q in range(PAIRS)]
-        scaled = [[keep.tile([P, 2, P], F32, name=f"scaled{q}_{c}") for c in range(2 * D)] for q in range(PAIRS)]
+        turned = [[None, None] for q in range(PAIRS)]
+        scaled = [
+            [
+                keep.tile([P, 2 * P], BF16 if WORDS[q // 2][c % 2] and c >= 4 else F32, name=f"scaled{q}_{c}")
+                for c in range(2 * D)
+            ]
+            for q in range(PAIRS)
+        ]
         sums = [[None, None] for a in range(PASSES)]
         x_bf = [keep.tile([P, V, 4], BF16, name=f"x_bf{a}", align_bytes=64) for a in range(PASSES)]
         x_codes = [keep.tile([P, V], U32, name=f"x_codes{a}", align_bytes=64) for a in range(PASSES)]
         x_plane = [keep.tile([P, V], U8, name=f"x_plane{a}", align_bytes=64) for a in range(PASSES)]
 
         def cast(q):
+            if q == 0:
+                for i in range(2):
+                    nc.vector.tensor_copy(
+                        pairs[0][:, i * T // 2 : (i + 1) * T // 2, :], first[i][:].rearrange("p e t -> p t e")
+                    )
+                return
             src = raw[q][:].rearrange("p e t -> p t e")
             if CAST[q] == "v":
                 nc.vector.tensor_copy(pairs[q][:], src)
@@ -85,95 +116,162 @@ def tile_picked_bag_lin_bias_sub_l_kernel(tc, xT, w_words, w_scales, b, gate, of
             else:
                 nc.gpsimd.tensor_scalar(pairs[q][:], src, 1.0, 0.0, MULT, ADD)
 
-        def gather(q):
+        def gather(q, s):
             window = pairs[q][:].rearrange("p t e -> p (t e)").bitcast(U32)
-            for s in range(2):
-                nc.vector.tensor_copy(picked[q][s][:], window.indirect(offsets[:, 24 * s : 24 * s + 24]))
+            nc.vector.tensor_copy(picked[q][s][:], window.indirect(offsets[:, 24 * s : 24 * s + 24]))
 
-        def weigh(q):
-            for s in range(2):
-                turned = turn.tile([P, 4, P], F32, name="turned")
-                for i in range(3):
-                    nc.tensor.transpose(turned[:, i, :], picked[q][s][:, P * i : P * (i + 1)].bitcast(F32), ident[:])
-                for i in range(3):
-                    c = 3 * s + i
-                    src = turned[:, i, :].bitcast(BF16).rearrange("v (p e) -> v e p", e=2)
-                    if SCALE[q][c] == "s":
-                        nc.scalar.activation(scaled[q][c][:], src, COPY, scale=cols[:, c : c + 1])
-                    elif SCALE[q][c] == "v":
-                        nc.vector.tensor_scalar(scaled[q][c][:], src, cols[:, c : c + 1], None, MULT)
-                    else:
-                        nc.vector.scalar_tensor_tensor(
-                            scaled[q][c][:], src, cols[:, c : c + 1], scaled[q][c - 2][:], MULT, ADD
-                        )
+        def turn(q, s):
+            turned[q][s] = bank(TURN_BANK[q][s])
+            for i in range(3):
+                nc.tensor.transpose(turned[q][s][:, i, :], picked[q][s][:, P * i : P * (i + 1)].bitcast(F32), ident[:])
+            for i in range(FILL[q][s]):
+                nc.tensor.transpose(turned[q][s][:, 3, :], picked[q][s][:, 0:P].bitcast(F32), ident[:])
 
-        def add_up(q):
+        def weigh(q, c):
+            src = turned[q][c // 3][:, c % 3, :].bitcast(BF16)
+            dst = scaled[q][c][:]
+            before = scaled[q][c - 2][:]
+            if not WORDS[q // 2][c % 2]:
+                src = src.rearrange("v (p e) -> v e p", e=2)
+                dst = dst.rearrange("v (e p) -> v e p", e=2)
+                before = before.rearrange("v (e p) -> v e p", e=2)
+            if SCALE[q][c] == "s":
+                nc.scalar.activation(dst, src, COPY, scale=cols[:, c : c + 1])
+            elif SCALE[q][c] == "v":
+                nc.vector.tensor_scalar(dst, src, cols[:, c : c + 1], None, MULT)
+            else:
+                nc.vector.scalar_tensor_tensor(dst, src, cols[:, c : c + 1], before, MULT, ADD)
+
+        def add_up(q, h, e):
             a, u = divmod(q, 2)
-            for h in range(2):
-                if u == 0:
-                    sums[a][h] = back.tile([P, 4, P], F32, name="sums")
-                terms = [d for d in range(D) if d == D - 1 or SCALE[q][2 * d + 2 + h] != "m"]
-                for e in range(2):
-                    for d in terms:
-                        nc.tensor.matmul(
-                            sums[a][h][:, 2 * u + e, :], scaled[q][2 * d + h][:, e, :], ident[:],
-                            start=(d == terms[0]), stop=(d == terms[-1]), is_transpose=True,
-                        )
+            if sums[a][h] is None:
+                sums[a][h] = bank(SUM_BANK[a][h])
+            if WORDS[a][h]:
+                nc.tensor.transpose(sums[a][h][:, u, :], scaled[q][4 + h][:].bitcast(F32), ident[:])
+                return
+            terms = [d for d in range(D) if d == D - 1 or SCALE[q][2 * d + 2 + h] != "m"]
+            for d in terms:
+                nc.tensor.matmul(
+                    sums[a][h][:, 2 * u + e, :], scaled[q][2 * d + h][:, P * e : P * (e + 1)], ident[:],
+                    start=(d == terms[0]), stop=(d == terms[-1]), is_transpose=True,
+                )
 
-        def round_sums(a):
-            nc.scalar.copy(x_bf[a][:, 0:P, :], sums[a][0][:].rearrange("p j v -> p v j"))
-            src = sums[a][1][:].rearrange("p j v -> p v j")
-            nc.vector.tensor_copy(x_bf[a][:, P:V, :], src)
+        def round_sums(a, h):
+            dst = x_bf[a][:, P * h : P * (h + 1), :]
+            if WORDS[a][h]:
+                dst = dst.bitcast(F32)
+                src = sums[a][h][:, 0:2, :].rearrange("p u v -> p v u")
+            else:
+                src = sums[a][h][:].rearrange("p j v -> p v j")
+            if ROUND[a][h] == "s":
+                nc.scalar.copy(dst, src)
+            else:
+                nc.vector.tensor_copy(dst, src)
 
-        def quantise(a):
+        def quantise(a, h, n):
+            cs = slice(P * h, P * (h + n))
             nc.vector.quantize_mx(
-                out=x_codes[a][:].bitcast(FP8X4), scales=x_plane[a][:], in_=x_bf[a][:].rearrange("p v j -> p (v j)")
+                out=x_codes[a][:, cs].bitcast(FP8X4), scales=x_plane[a][:, cs],
+                in_=x_bf[a][:, cs, :].rearrange("p v j -> p (v j)"),
             )
 
-        acc = [None] * 4
+        acc = [[None] * 4 for h in range(2)]
+        result = [keep.tile([P, 4, P], F32, name=f"result{h}") for h in range(2)]
+        out_rows = out.rearrange("(t p) v -> p t v", p=P)
 
-        def multiply(a):
+        def multiply(a, h, n):
+            cs = slice(P * h, P * (h + 1))
             for t in range(4):
                 if a == 0:
-                    acc[t] = turn.tile([P, 4, P], F32, name="turned")
+                    acc[h][t] = bank(ACC_BANK[h][t])
                 nc.tensor.matmul_mx(
-                    out=acc[t][:, 0:2, :].rearrange("p h v -> p (h v)"),
+                    out=acc[h][t][:, 0, :],
                     lhsT=w_codes[:, a, P * t : P * (t + 1)].bitcast(FP8X4),
                     lhsT_scale=w_plane[4 * a :, P * t : P * (t + 1)],
-                    rhs=x_codes[a][:].bitcast(FP8X4),
-                    rhs_scale=x_plane[a][:],
+                    rhs=x_codes[a][:, cs].bitcast(FP8X4),
+                    rhs_scale=x_plane[a][:, cs],
                     start=(a == 0),
                     stop=(a == PASSES - 1),
                 )
 
+        def finish(h):
+            for t in range(4):
+                bias = cols[:, BIAS_ROW + t : BIAS_ROW + t + 1]
+                if t % 2 == 0:
+                    nc.scalar.activation(result[h][:, t, :], acc[h][t][:, 0, :], IDENT, bias=bias)
+                else:
+                    nc.vector.tensor_scalar(result[h][:, t, :], acc[h][t][:, 0, :], bias, None, ADD)
+                if t % 2 == 1:
+                    ts = slice(t - 1, t + 1)
+                    nc.sync.dma_start(out_rows[:, ts, P * h : P * (h + 1)], result[h][:, ts, :])
+
         cast(0)
-        gather(0)
+        gather(0, 0)
         cast(1)
-        gather(1)
+        gather(0, 1)
+        turn(0, 0)
         cast(2)
-        gather(2)
+        gather(1, 0)
+        turn(0, 1)
+        weigh(0, 0)
+        gather(1, 1)
+        weigh(0, 2)
+        turn(1, 0)
+        weigh(0, 4)
+        add_up(0, 0, 1)
         cast(3)
-        gather(3)
-        weigh(0)
-        weigh(1)
-        weigh(2)
-        weigh(3)
-        add_up(0)
-        add_up(1)
-        add_up(2)
-        round_sums(0)
-        add_up(3)
-        quantise(0)
-        multiply(0)
-        round_sums(1)
-        quantise(1)
-        multiply(1)
-        for t in range(4):
-            result = keep.tile([P, V], F32, name=f"result{t}")
-            src = acc[t][:, 0:2, :].rearrange("p h v -> p (h v)")
-            bias = cols[:, BIAS_ROW + t : BIAS_ROW + t + 1]
-            if t % 2 == 0:
-                nc.scalar.activation(result[:], src, IDENT, bias=bias)
-            else:
-                nc.vector.tensor_scalar(result[:], src, bias, None, ADD)
-            nc.sync.dma_start(out[P * t : P * (t + 1), :], result[:])
+        gather(2, 0)
+        turn(1, 1)
+        add_up(0, 0, 0)
+        gather(2, 1)
+        weigh(1, 0)
+        turn(2, 0)
+        weigh(0, 1)
+        weigh(1, 1)
+        gather(3, 0)
+        weigh(1, 2)
+        turn(2, 1)
+        weigh(1, 4)
+        add_up(1, 0, 0)
+        weigh(2, 0)
+        gather(3, 1)
+        weigh(2, 2)
+        turn(3, 0)
+        weigh(2, 1)
+        add_up(1, 0, 1)
+        weigh(2, 4)
+        weigh(1, 3)
+        weigh(3, 0)
+        turn(3, 1)
+        weigh(0, 3)
+        weigh(3, 1)
+        weigh(1, 5)
+        add_up(2, 0, 0)
+        weigh(3, 2)
+        weigh(0, 5)
+        round_sums(0, 0)
+        add_up(1, 1, 0)
+        weigh(2, 3)
+        add_up(0, 1, 0)
+        weigh(3, 4)
+        add_up(2, 0, 1)
+        weigh(3, 3)
+        add_up(3, 0, 1)
+        weigh(2, 5)
+        add_up(3, 0, 0)
+        weigh(3, 5)
+        add_up(2, 1, 0)
+        quantise(0, 0, 1)
+        round_sums(0, 1)
+        round_sums(1, 0)
+        add_up(3, 1, 0)
+        multiply(0, 0, 1)
+        quantise(0, 1, 1)
+        round_sums(1, 1)
+        quantise(1, 0, 1)
+        multiply(0, 1, 1)
+        quantise(1, 1, 1)
+        multiply(1, 0, 1)
+        finish(0)
+        multiply(1, 1, 1)
+        finish(1)

from contextlib import ExitStack

import concourse.mybir as mybir
from concourse.masks import make_identity

K, T, D, V, N = 1024, 512, 3, 256, 512
FLOPS = 2 * K * N * V

F32 = mybir.dt.float32
BF16 = mybir.dt.bfloat16
I32 = mybir.dt.int32
U32 = mybir.dt.uint32
U16 = mybir.dt.uint16
U8 = mybir.dt.uint8
FP8X4 = mybir.dt.float8_e4m3fn_x4
COPY = mybir.ActivationFunctionType.Copy
IDENT = mybir.ActivationFunctionType.Identity
MULT = mybir.AluOpType.mult
ADD = mybir.AluOpType.add

P = 128
PASSES = 2
PAIRS = 4
PIECE = 384
BIAS_ROW = 8
CAST = "vsss"
SCALE = ["sssmsm","sssmsm","sssmsm","sssmmm"]
WORDS = [[0,1],[0,1]]
ROUND = ["sv","ss"]
TURN_BANK = [[0,1],[2,4],[5,6],[7,0]]
SUM_BANK = [[3,5],[2,4]]
ACC_BANK = [[7,1,3,6],[0,5,2,4]]
WARM_BANK = 7
WARM_UP = 20
FILL = [[2,2],[2,0],[0,0],[0,0]]
N_MULTIPLY = 4


def tile_picked_bag_lin_bias_sub_l_kernel(tc, xT, w_words, w_scales, b, gate, offs, out):
    nc = tc.nc
    with ExitStack() as ctx:
        keep = ctx.enter_context(tc.tile_pool(name="keep", bufs=1))
        psum = ctx.enter_context(tc.psum_pool(name="psum", bufs=1))

        def bank(i):
            return psum.tile([P, 4, P], F32, name=f"bank{i}")

        offsets = keep.tile([P, D * V // 16], U16, name="offsets")
        x_rows = xT.rearrange("(a p u e) t -> a u p e t", a=PASSES, p=P, u=2, e=2)
        first = [keep.tile([P, 2, T // 2], F32, name=f"first{i}") for i in range(2)]
        for i in range(2):
            nc.sync.dma_start(first[i][:], x_rows[0, 0][:, :, i * T // 2 : (i + 1) * T // 2])
        nc.sync.dma_start(offsets[:], offs)
        rows = keep.tile([P, P], F32, name="rows")
        nc.vector.memset(rows[:], 0.0)
        gate_rows = gate[:, 0, :].rearrange("d (h v) -> d h v", h=2)
        raw = [None] + [keep.tile([P, 2, T], F32, name=f"raw{q}") for q in range(1, PAIRS)]
        nc.sync.dma_start(raw[1][:], x_rows[0, 1])
        nc.sync.dma_start(rows[0:4, :], gate_rows[0:2])
        nc.sync.dma_start(rows[4:6, :], gate_rows[2])
        nc.sync.dma_start(rows[BIAS_ROW : BIAS_ROW + 4, :], b.rearrange("(t p) o -> t (p o)", p=P))
        for q in range(2, PAIRS):
            nc.sync.dma_start(raw[q][:], x_rows[q // 2, q % 2])

        ident = keep.tile([P, P], F32, name="ident")
        make_identity(nc, ident[:])
        w_plane = keep.tile([P, N], U8, name="w_plane", align_bytes=64)
        nc.gpsimd.memset(w_plane[:].bitcast(U32), 0)

        warm = keep.tile([P, 8], F32, name="warm")
        nc.vector.memset(warm[:, 0:4], 0.0)
        nc.scalar.activation(warm[:, 4:8], warm[:, 0:4], IDENT)

        w_codes = keep.tile([P, PASSES, N], U32, name="w_codes", align_bytes=64)
        nc.sync.dma_start(w_codes[:].bitcast(I32), w_words.rearrange("a p n t -> p a (n t)").bitcast(I32))
        for quad in range(4):
            nc.sync.dma_start(
                w_plane[32 * quad : 32 * quad + 8, :].bitcast(I32),
                w_scales[:, 4 * quad : 4 * quad + 4, :].bitcast(I32),
            )

        rows_turned = bank(WARM_BANK)
        for i in range(WARM_UP):
            nc.tensor.transpose(rows_turned[:, 1 + i % 3, :], ident[:], ident[:])
        nc.tensor.transpose(rows_turned[:, 0, :], rows[:], ident[:])
        cols = keep.tile([P, 16], F32, name="cols")
        nc.scalar.copy(cols[:], rows_turned[:, 0, 0:16])

        pairs = [keep.tile([P, T, 2], BF16, name=f"pairs{q}") for q in range(PAIRS)]
        picked = [[keep.tile([P, PIECE], U32, name=f"picked{q}_{s}") for s in range(2)] for q in range(PAIRS)]
        turned = [[None, None] for q in range(PAIRS)]
        scaled = [
            [
                keep.tile([P, 2 * P], BF16 if WORDS[q // 2][c % 2] and c >= 4 else F32, name=f"scaled{q}_{c}")
                for c in range(2 * D)
            ]
            for q in range(PAIRS)
        ]
        sums = [[None, None] for a in range(PASSES)]
        x_bf = [keep.tile([P, V, 4], BF16, name=f"x_bf{a}", align_bytes=64) for a in range(PASSES)]
        x_codes = [keep.tile([P, V], U32, name=f"x_codes{a}", align_bytes=64) for a in range(PASSES)]
        x_plane = [keep.tile([P, V], U8, name=f"x_plane{a}", align_bytes=64) for a in range(PASSES)]

        def cast(q):
            if q == 0:
                for i in range(2):
                    nc.vector.tensor_copy(
                        pairs[0][:, i * T // 2 : (i + 1) * T // 2, :], first[i][:].rearrange("p e t -> p t e")
                    )
                return
            src = raw[q][:].rearrange("p e t -> p t e")
            if CAST[q] == "v":
                nc.vector.tensor_copy(pairs[q][:], src)
            elif CAST[q] == "s":
                nc.scalar.copy(pairs[q][:], src)
            else:
                nc.gpsimd.tensor_scalar(pairs[q][:], src, 1.0, 0.0, MULT, ADD)

        def gather(q, s):
            window = pairs[q][:].rearrange("p t e -> p (t e)").bitcast(U32)
            nc.vector.tensor_copy(picked[q][s][:], window.indirect(offsets[:, 24 * s : 24 * s + 24]))

        def turn(q, s):
            turned[q][s] = bank(TURN_BANK[q][s])
            for i in range(3):
                nc.tensor.transpose(turned[q][s][:, i, :], picked[q][s][:, P * i : P * (i + 1)].bitcast(F32), ident[:])
            for i in range(FILL[q][s]):
                nc.tensor.transpose(turned[q][s][:, 3, :], picked[q][s][:, 0:P].bitcast(F32), ident[:])

        def weigh(q, c):
            src = turned[q][c // 3][:, c % 3, :].bitcast(BF16)
            dst = scaled[q][c][:]
            before = scaled[q][c - 2][:]
            if not WORDS[q // 2][c % 2]:
                src = src.rearrange("v (p e) -> v e p", e=2)
                dst = dst.rearrange("v (e p) -> v e p", e=2)
                before = before.rearrange("v (e p) -> v e p", e=2)
            if SCALE[q][c] == "s":
                nc.scalar.activation(dst, src, COPY, scale=cols[:, c : c + 1])
            elif SCALE[q][c] == "v":
                nc.vector.tensor_scalar(dst, src, cols[:, c : c + 1], None, MULT)
            else:
                nc.vector.scalar_tensor_tensor(dst, src, cols[:, c : c + 1], before, MULT, ADD)

        def add_up(q, h, e):
            a, u = divmod(q, 2)
            if sums[a][h] is None:
                sums[a][h] = bank(SUM_BANK[a][h])
            if WORDS[a][h]:
                nc.tensor.transpose(sums[a][h][:, u, :], scaled[q][4 + h][:].bitcast(F32), ident[:])
                return
            terms = [d for d in range(D) if d == D - 1 or SCALE[q][2 * d + 2 + h] != "m"]
            for d in terms:
                nc.tensor.matmul(
                    sums[a][h][:, 2 * u + e, :], scaled[q][2 * d + h][:, P * e : P * (e + 1)], ident[:],
                    start=(d == terms[0]), stop=(d == terms[-1]), is_transpose=True,
                )

        def round_sums(a, h):
            dst = x_bf[a][:, P * h : P * (h + 1), :]
            if WORDS[a][h]:
                dst = dst.bitcast(F32)
                src = sums[a][h][:, 0:2, :].rearrange("p u v -> p v u")
            else:
                src = sums[a][h][:].rearrange("p j v -> p v j")
            if ROUND[a][h] == "s":
                nc.scalar.copy(dst, src)
            else:
                nc.vector.tensor_copy(dst, src)

        def quantise(a, h, n):
            cs = slice(P * h, P * (h + n))
            nc.vector.quantize_mx(
                out=x_codes[a][:, cs].bitcast(FP8X4), scales=x_plane[a][:, cs],
                in_=x_bf[a][:, cs, :].rearrange("p v j -> p (v j)"),
            )

        acc = [[None] * 4 for h in range(2)]
        result = [keep.tile([P, 4, P], F32, name=f"result{h}") for h in range(2)]
        out_rows = out.rearrange("(t p) v -> p t v", p=P)

        def multiply(a, h, n):
            cs = slice(P * h, P * (h + 1))
            for t in range(4):
                if a == 0:
                    acc[h][t] = bank(ACC_BANK[h][t])
                nc.tensor.matmul_mx(
                    out=acc[h][t][:, 0, :],
                    lhsT=w_codes[:, a, P * t : P * (t + 1)].bitcast(FP8X4),
                    lhsT_scale=w_plane[4 * a :, P * t : P * (t + 1)],
                    rhs=x_codes[a][:, cs].bitcast(FP8X4),
                    rhs_scale=x_plane[a][:, cs],
                    start=(a == 0),
                    stop=(a == PASSES - 1),
                )

        def finish(h):
            for t in range(4):
                bias = cols[:, BIAS_ROW + t : BIAS_ROW + t + 1]
                if t % 2 == 0:
                    nc.scalar.activation(result[h][:, t, :], acc[h][t][:, 0, :], IDENT, bias=bias)
                else:
                    nc.vector.tensor_scalar(result[h][:, t, :], acc[h][t][:, 0, :], bias, None, ADD)
                if t % 2 == 1:
                    ts = slice(t - 1, t + 1)
                    nc.sync.dma_start(out_rows[:, ts, P * h : P * (h + 1)], result[h][:, ts, :])

        cast(0)
        gather(0, 0)
        cast(1)
        gather(0, 1)
        turn(0, 0)
        cast(2)
        gather(1, 0)
        turn(0, 1)
        weigh(0, 0)
        gather(1, 1)
        weigh(0, 2)
        turn(1, 0)
        weigh(0, 4)
        add_up(0, 0, 1)
        cast(3)
        gather(2, 0)
        turn(1, 1)
        add_up(0, 0, 0)
        gather(2, 1)
        weigh(1, 0)
        turn(2, 0)
        weigh(0, 1)
        weigh(1, 1)
        gather(3, 0)
        weigh(1, 2)
        turn(2, 1)
        weigh(1, 4)
        add_up(1, 0, 0)
        weigh(2, 0)
        gather(3, 1)
        weigh(2, 2)
        turn(3, 0)
        weigh(2, 1)
        add_up(1, 0, 1)
        weigh(2, 4)
        weigh(1, 3)
        weigh(3, 0)
        turn(3, 1)
        weigh(0, 3)
        weigh(3, 1)
        weigh(1, 5)
        add_up(2, 0, 0)
        weigh(3, 2)
        weigh(0, 5)
        round_sums(0, 0)
        add_up(1, 1, 0)
        weigh(2, 3)
        add_up(0, 1, 0)
        weigh(3, 4)
        add_up(2, 0, 1)
        weigh(3, 3)
        add_up(3, 0, 1)
        weigh(2, 5)
        add_up(3, 0, 0)
        weigh(3, 5)
        add_up(2, 1, 0)
        quantise(0, 0, 1)
        round_sums(0, 1)
        round_sums(1, 0)
        add_up(3, 1, 0)
        multiply(0, 0, 1)
        quantise(0, 1, 1)
        round_sums(1, 1)
        quantise(1, 0, 1)
        multiply(0, 1, 1)
        quantise(1, 1, 1)
        multiply(1, 0, 1)
        finish(0)
        multiply(1, 1, 1)
        finish(1)
